import numpy as np
import ml_dtypes


def mxq(x, axis, fmt="e4m3"):
    dtype, down = {"e4m3": (ml_dtypes.float8_e4m3fn, 7), "e5m2": (ml_dtypes.float8_e5m2, 14)}[fmt]
    v = np.moveaxis(np.asarray(x, np.float32).astype(ml_dtypes.bfloat16).astype(np.float64), axis, -1)
    blocks = v.reshape(v.shape[:-1] + (-1, 32))
    amax = np.abs(blocks).max(-1, keepdims=True)
    byte = np.maximum(np.where(amax > 0, np.frexp(amax)[1] - 1 + 127, 0) - down, 1)
    scale = np.exp2(byte - 127.0)
    codes = (blocks / scale).astype(np.float32).astype(dtype).astype(np.float64)
    return np.moveaxis((codes * scale).reshape(v.shape), -1, axis)


WIDE = False


def mx_kscale(k):
    if not WIDE:
        return np.ones(k)
    levels = np.array([10, -10, 5, -5, 0])
    if k % 512:
        return np.exp2(np.random.permutation(np.resize(levels, k // 32))).repeat(32)
    a = np.empty((k // 512, 16))
    for p in range(k // 512):
        a[p, :8] = np.random.permutation(np.resize(levels, 8))
        for g in range(8):
            far = levels[np.abs(levels - a[p, g]) >= 10]
            a[p, g + 8] = far[np.random.randint(len(far))]
    return np.exp2(a.ravel()).repeat(32)


def f64(x):
    return np.asarray(x).astype(np.float64)


def striped(idx):
    return np.tile(idx.reshape(-1, 16).T, (8, 1)).astype(np.uint16)


def unstriped(offs):
    return offs[:16].T.reshape(-1).astype(np.int64)


def striped8(idx):
    return np.concatenate([x.reshape(-1, 16).T for x in idx]).astype(np.uint16)


def runs(offs, k):
    lists = np.stack([offs[16 * r : 16 * r + 16].T.reshape(-1) for r in range(8)]).astype(np.int64)
    return lists[np.arange(k) % 512 // 64]


def pack_weight(w):
    k, n = w.shape
    w = f64(np.asarray(w, np.float32).astype(ml_dtypes.bfloat16)).reshape(k // 32, 32, n)
    amax = np.abs(w).max(1)
    byte = np.clip(np.where(amax > 0, np.frexp(amax)[1] - 1 + 127 - 7, 1), 1, 254)
    scaled = (w * np.exp2(127.0 - byte)[:, None, :]).reshape(k, n).astype(np.float32)
    words = np.ascontiguousarray(scaled.reshape(k // 512, 128, 4, n).transpose(0, 1, 3, 2)).astype(ml_dtypes.float8_e4m3fn).view(np.uint8)
    return words, np.ascontiguousarray(byte.astype(np.uint8).reshape(k // 512, 16, n))


def unpack_weight(words, scales):
    g, p, n, _ = words.shape
    vals = np.ascontiguousarray(words).view(ml_dtypes.float8_e4m3fn).astype(np.float64) * np.repeat(np.exp2(scales.astype(np.float64) - 127.0), 8, axis=1)[..., None]
    return vals.transpose(0, 1, 3, 2).reshape(g * 512, n)


def sigmoid(v):
    return 1.0 / (1.0 + np.exp(-np.maximum(v, -700.0)))

def planes(y):
    n, m = y.shape
    v = y.astype(np.float32).astype(ml_dtypes.bfloat16).astype(np.float64).reshape(n // 32, 32, m)
    top = np.abs(v).max(1)
    byte = np.clip(np.where(top > 0, np.frexp(top)[1] - 1 + 127 - 7, 1), 1, 254)
    codes = (v * np.exp2(127.0 - byte)[:, None, :]).reshape(n, m).astype(np.float32).astype(ml_dtypes.float8_e4m3fn).view(np.uint8)
    words = codes.reshape(n // 512, 128, 4, m).transpose(0, 1, 3, 2)
    return np.ascontiguousarray(words), np.ascontiguousarray(byte.astype(np.uint8).reshape(n // 512, 16, m))


K, T, S, V, H, W = 512, 2048, 512, 512, 512, 256


def setup_inputs():
    n = np.random.standard_normal
    s = mx_kscale(K)[:, None]
    u = mx_kscale(S)
    packed_xT = pack_weight(n((K, T)) * s)
    packed_w1 = pack_weight(n((K, H)) / np.sqrt(K) / s)
    packed_w2 = pack_weight(n((K, H)) / np.sqrt(K) / s)
    perm = np.stack([np.random.permutation(S) for _ in range(8)])
    return {
        "x_words": packed_xT[0],
        "x_scales": packed_xT[1],
        "w1_words": packed_w1[0],
        "w1_scales": packed_w1[1],
        "w2_words": packed_w2[0],
        "w2_scales": packed_w2[1],
        "ga": (np.random.uniform(0.5, 1.5, (H, 1)) * u[:, None]).astype(np.float32),
        "gb": (np.random.uniform(0.5, 1.5, (H, 1)) / u[:, None]).astype(np.float32),
        "offs": striped(np.random.permutation(T)[:S]),
        "two": striped(np.random.permutation(T)[:V]),
        "n1": striped8(perm[:, :W]),
        "n2": striped8(perm[:, W:]),
        "n3": striped8(np.stack([np.random.permutation(V) for _ in range(8)])),
        "n4": striped8(np.stack([np.random.permutation(V) for _ in range(8)])),
        "n5": striped8(np.stack([np.random.permutation(V) for _ in range(8)])),
        "n6": striped8(np.stack([np.random.permutation(V) for _ in range(8)])),
    }


def reference(x_words, x_scales, w1_words, w1_scales, w2_words, w2_scales, ga, gb, offs, two, n1, n2, n3, n4, n5, n6):
    xq = unpack_weight(x_words, x_scales)[:, unstriped(offs)]
    a = unpack_weight(w1_words, w1_scales).T @ xq
    pa = a[np.arange(H)[:, None], runs(n1, H)]
    pb = a[np.arange(H)[:, None], runs(n2, H)]
    rb = np.maximum(pa, pb)
    ra = pa / (np.abs(pb) + 0.5)
    ds = np.zeros((H, S))
    ds[np.arange(H)[:, None], runs(n1, H)] = ra
    dt = ds.copy()
    dt[np.arange(H)[:, None], runs(n2, H)] = rb
    z = f64(ga) * dt
    x_two = unpack_weight(x_words, x_scales)[:, unstriped(two)]
    b = unpack_weight(w2_words, w2_scales).T @ x_two
    z2 = f64(gb) * (np.maximum(b[np.arange(H)[:, None], runs(n3, H)], b[np.arange(H)[:, None], runs(n4, H)]) - (0.75 * b))
    s = 0.0625 * ((mxq(z, 0, "e4m3").T @ mxq(z2, 0, "e4m3")))
    out_0 = s * (sigmoid(s[np.arange(S)[:, None], runs(n5, S)] - (s[np.arange(S)[:, None], runs(n6, S)])))
    return (out_0,) + planes(out_0)

@@ -1,0 +1,202 @@
+from contextlib import ExitStack
+
+import concourse.mybir as mybir
+
+K, T, S, V, H, W = 512, 2048, 512, 512, 512, 256
+FLOPS = 3 * 2 * 512 * 512 * 512
+
+F32 = mybir.dt.float32
+BF16 = mybir.dt.bfloat16
+I32 = mybir.dt.int32
+U32 = mybir.dt.uint32
+U16 = mybir.dt.uint16
+U8 = mybir.dt.uint8
+FP8X4 = mybir.dt.float8_e4m3fn_x4
+ACT = mybir.ActivationFunctionType
+ALU = mybir.AluOpType
+
+P = 128
+PACK = 4
+OUT_CHUNKS = ((0, 256), (256, 128), (384, 128))
+B_CHUNK = 256
+
+
+def tile_picked_kqratioovercmp_none_po_kernel(
+    tc, x_words, x_scales, w1_words, w1_scales, w2_words, w2_scales, ga, gb,
+    offs, two, n1, n2, n3, n4, n5, n6, out_0, out_1, out_2,
+):
+    nc = tc.nc
+    with ExitStack() as ctx:
+        lists = ctx.enter_context(tc.tile_pool(name="lists", bufs=1))
+        keep = ctx.enter_context(tc.tile_pool(name="keep", bufs=1))
+        psum = ctx.enter_context(tc.psum_pool(name="psum", bufs=8))
+
+        def sb(name, shape, dtype):
+            return keep.tile(shape, dtype, name=name, align_bytes=64)
+
+        def load_list(name, src):
+            t = lists.tile(list(src.shape), U16, name=name)
+            nc.sync.dma_start(t[:], src)
+            return t
+
+        def load_words(t, src):
+            nc.sync.dma_start(t[:].bitcast(I32), src[0].rearrange("p n r -> p (n r)").bitcast(I32))
+
+        def load_scales(t, src, queue):
+            for q in range(4):
+                queue.dma_start(t[32 * q : 32 * q + 4, :].bitcast(I32), src[0, 4 * q : 4 * q + 4, :].bitcast(I32))
+
+        def load_gain(name, src):
+            t = sb(name, [P, PACK], F32)
+            nc.gpsimd.dma_start(t[:], src.rearrange("(p t) o -> p (t o)", t=PACK))
+            return t
+
+        xw = sb("xw", [P, T], U32)
+        xs = sb("xs", [P, T], U8)
+        w1w = sb("w1w", [P, H], U32)
+        w1s = sb("w1s", [P, H], U8)
+        w2w = sb("w2w", [P, H], U32)
+        w2s = sb("w2s", [P, H], U8)
+        nc.gpsimd.memset(xs[:].bitcast(I32), 0)
+        nc.gpsimd.memset(w1s[:].bitcast(I32), 0)
+        nc.gpsimd.memset(w2s[:].bitcast(I32), 0)
+        load_words(xw, x_words)
+        load_scales(xs, x_scales, nc.scalar)
+        offs_t = load_list("offs_t", offs)
+        load_words(w1w, w1_words)
+        two_t = load_list("two_t", two)
+        load_scales(w1s, w1_scales, nc.scalar)
+        n2_t = load_list("n2_t", n2)
+        n1_t = load_list("n1_t", n1)
+        load_words(w2w, w2_words)
+        load_scales(w2s, w2_scales, nc.sync)
+        n3_t = load_list("n3_t", n3)
+        n4_t = load_list("n4_t", n4)
+        n6_t = load_list("n6_t", n6)
+        n5_t = load_list("n5_t", n5)
+        gb_t = load_gain("gb_t", gb)
+        ga_t = load_gain("ga_t", ga)
+        half = sb("half", [P, 1], F32)
+        nc.gpsimd.memset(half[:], 0.5)
+
+        def deal(name, words, scales):
+            dw = sb(name + "_dw", [P, PACK, P], U32)
+            ds = sb(name + "_ds", [P, PACK, P], U8)
+            nc.vector.tensor_copy(
+                dw[:].bitcast(I32).rearrange("p t m -> p m t"),
+                words[:].bitcast(I32).rearrange("p (m t) -> p m t", t=PACK),
+            )
+            nc.vector.tensor_copy(
+                ds[:].rearrange("p t m -> p m t"), scales[:].rearrange("p (m t) -> p m t", t=PACK)
+            )
+            return dw, ds
+
+        def pick(name, lst):
+            gs = sb(name + "_gs", [P, S], U8)
+            gw = sb(name + "_gw", [P, S], U32)
+            nc.vector.tensor_copy(gs[:], xs[:].indirect(lst[:]))
+            nc.vector.tensor_copy(gw[:], xw[:].indirect(lst[:]))
+            return gw, gs
+
+        def product(lw, ls, rw, rs):
+            acc = psum.tile([P, 512], F32, name="acc")
+            nc.tensor.matmul_mx(
+                out=acc[:], lhsT=lw.bitcast(FP8X4), lhsT_scale=ls, rhs=rw.bitcast(FP8X4), rhs_scale=rs,
+                start=True, stop=True,
+            )
+            return acc
+
+        w1dw, w1ds = deal("w1", w1w, w1s)
+        xaw, xas = pick("xa", offs_t)
+        xbw, xbs = pick("xb", two_t)
+        w2dw, w2ds = deal("w2", w2w, w2s)
+
+        a = []
+        for t in range(PACK):
+            acc = product(w1dw[:, t, :], w1ds[:, t, :], xaw[:], xas[:])
+            a.append(sb(f"a{t}", [P, S], F32))
+            nc.scalar.copy(a[t][:], acc[:])
+        b, c = [], []
+        for t in range(PACK):
+            acc = product(w2dw[:, t, :], w2ds[:, t, :], xbw[:], xbs[:])
+            b.append(sb(f"b{t}", [P, V], F32))
+            c.append(sb(f"c{t}", [P, V], F32))
+            nc.scalar.copy(b[t][:], acc[:])
+            nc.scalar.activation(c[t][:], acc[:], ACT.Copy, scale=-0.75)
+
+        pa = sb("pa", [P, PACK, W], F32)
+        pb = sb("pb", [P, PACK, W], F32)
+        for t in range(PACK):
+            nc.vector.tensor_copy(pb[:, t, :], a[t][:].indirect(n2_t[:]))
+            nc.vector.tensor_copy(pa[:, t, :], a[t][:].indirect(n1_t[:]))
+        rb = sb("rb", [P, PACK, W], F32)
+        nc.vector.tensor_tensor(rb[:], pa[:], pb[:], ALU.max)
+        size = sb("size", [P, PACK, W], F32)
+        logd = sb("logd", [P, PACK, W], F32)
+        rec = sb("rec", [P, PACK, W], F32)
+        nc.scalar.activation(size[:], pb[:], ACT.Abs)
+        nc.scalar.activation(logd[:], size[:], ACT.Ln, bias=half[:])
+        nc.scalar.activation(rec[:], logd[:], ACT.Exp, scale=-1.0)
+
+        z2b = sb("z2b", [P, V, PACK], BF16)
+        for t in range(PACK):
+            h3 = sb(f"h3_{t}", [P, V], F32)
+            h4 = sb(f"h4_{t}", [P, V], F32)
+            for v0 in range(0, V, B_CHUNK):
+                cols = slice(v0, v0 + B_CHUNK)
+                lc = slice(v0 // 16, (v0 + B_CHUNK) // 16)
+                nc.vector.tensor_tensor(h3[:, cols], b[t][:].indirect(n3_t[:, lc]), c[t][:, cols], ALU.add)
+                nc.vector.tensor_tensor(h4[:, cols], b[t][:].indirect(n4_t[:, lc]), c[t][:, cols], ALU.add)
+            m = sb(f"m{t}", [P, V], F32)
+            nc.vector.tensor_tensor(m[:], h3[:], h4[:], ALU.max)
+            nc.scalar.activation(z2b[:, :, t], m[:], ACT.Copy, scale=gb_t[:, t : t + 1])
+        z2w = sb("z2w", [P, V], U32)
+        z2s = sb("z2s", [P, V], U8)
+        nc.vector.quantize_mx(out=z2w[:].bitcast(FP8X4), scales=z2s[:], in_=z2b[:].rearrange("p v t -> p (v t)"))
+
+        zb = [sb(f"zb{u}", [P, P, PACK], BF16) for u in range(PACK)]
+        for t in range(PACK):
+            dt = sb(f"dt{t}", [P, S], F32)
+            nc.vector.tensor_copy(dt[:].indirect(n2_t[:]), rb[:, t, :])
+            nc.vector.tensor_tensor(dt[:].indirect(n1_t[:]), pa[:, t, :], rec[:, t, :], ALU.mult)
+            for u in range(PACK):
+                nc.scalar.activation(
+                    zb[u][:, :, t], dt[:].rearrange("p (m u) -> p u m", u=PACK)[:, u, :], ACT.Copy,
+                    scale=ga_t[:, t : t + 1],
+                )
+
+        sh = []
+        for u in range(PACK):
+            zw = sb(f"zw{u}", [P, P], U32)
+            zs = sb(f"zs{u}", [P, P], U8)
+            nc.vector.quantize_mx(out=zw[:].bitcast(FP8X4), scales=zs[:], in_=zb[u][:].rearrange("p m t -> p (m t)"))
+            acc = product(zw[:], zs[:], z2w[:], z2s[:])
+            sh.append(sb(f"sh{u}", [P, V], F32))
+            nc.scalar.activation(sh[u][:], acc[:], ACT.Copy, scale=0.03125)
+
+        out_rows = out_0.rearrange("(p u) v -> p u v", u=PACK)
+        out_words = out_1[0].rearrange("p v r -> p (v r)").bitcast(I32)
+        os_t = sb("os_t", [P, V], U8)
+        for v0, n in OUT_CHUNKS:
+            cols = slice(v0, v0 + n)
+            lc = slice(v0 // 16, (v0 + n) // 16)
+            o = sb(f"o{v0}", [P, PACK, n], F32)
+            for u in range(PACK):
+                g6 = sb(f"g6_{v0}_{u}", [P, n], F32)
+                d = sb(f"d_{v0}_{u}", [P, n], F32)
+                th = sb(f"th_{v0}_{u}", [P, n], F32)
+                nc.vector.tensor_copy(g6[:], sh[u][:].indirect(n6_t[:, lc]))
+                nc.vector.tensor_tensor(d[:], sh[u][:].indirect(n5_t[:, lc]), g6[:], ALU.subtract)
+                nc.scalar.activation(th[:], d[:], ACT.Tanh)
+                nc.vector.scalar_tensor_tensor(o[:, u, :], th[:], 1.0, sh[u][:, cols], ALU.add, ALU.mult)
+            nc.sync.dma_start(out_rows[:, :, cols], o[:])
+            ob = sb(f"ob{v0}", [P, n, PACK], BF16)
+            nc.scalar.copy(
+                ob[:].rearrange("p (c i) u -> p c u i", i=4), o[:].rearrange("p u (c i) -> p c u i", i=4)
+            )
+            ow = sb(f"ow{v0}", [P, n], U32)
+            nc.vector.quantize_mx(out=ow[:].bitcast(FP8X4), scales=os_t[:, cols], in_=ob[:].rearrange("p v u -> p (v u)"))
+            nc.sync.dma_start(out_words[:, cols], ow[:].bitcast(I32))
+        for q in range(4):
+            queue = nc.scalar if q % 2 else nc.sync
+            queue.dma_start(out_2[0, 4 * q : 4 * q + 4, :].bitcast(I32), os_t[32 * q : 32 * q + 4, :].bitcast(I32))

@@ -1,6 +1,7 @@
 from contextlib import ExitStack
 
 import concourse.mybir as mybir
+from concourse.masks import make_identity
 
 K, T, S, V, H, W = 512, 2048, 512, 512, 512, 256
 FLOPS = 3 * 2 * 512 * 512 * 512
@@ -31,8 +32,8 @@ def tile_picked_kqratioovercmp_none_po_kernel(
         keep = ctx.enter_context(tc.tile_pool(name="keep", bufs=1))
         psum = ctx.enter_context(tc.psum_pool(name="psum", bufs=8))
 
-        def sb(name, shape, dtype):
-            return keep.tile(shape, dtype, name=name, align_bytes=64)
+        def sb(name, shape, dtype, tag=None):
+            return keep.tile(shape, dtype, name=name, tag=tag or name, align_bytes=64)
 
         def load_list(name, src):
             t = lists.tile(list(src.shape), U16, name=name)
@@ -46,11 +47,6 @@ def tile_picked_kqratioovercmp_none_po_kernel(
             for q in range(4):
                 queue.dma_start(t[32 * q : 32 * q + 4, :].bitcast(I32), src[0, 4 * q : 4 * q + 4, :].bitcast(I32))
 
-        def load_gain(name, src):
-            t = sb(name, [P, PACK], F32)
-            nc.gpsimd.dma_start(t[:], src.rearrange("(p t) o -> p (t o)", t=PACK))
-            return t
-
         xw = sb("xw", [P, T], U32)
         xs = sb("xs", [P, T], U8)
         w1w = sb("w1w", [P, H], U32)
@@ -60,12 +56,12 @@ def tile_picked_kqratioovercmp_none_po_kernel(
         nc.gpsimd.memset(xs[:].bitcast(I32), 0)
         nc.gpsimd.memset(w1s[:].bitcast(I32), 0)
         nc.gpsimd.memset(w2s[:].bitcast(I32), 0)
-        load_words(xw, x_words)
-        load_scales(xs, x_scales, nc.scalar)
         offs_t = load_list("offs_t", offs)
-        load_words(w1w, w1_words)
         two_t = load_list("two_t", two)
-        load_scales(w1s, w1_scales, nc.scalar)
+        load_words(w1w, w1_words)
+        load_scales(xs, x_scales, nc.sync)
+        load_words(xw, x_words)
+        load_scales(w1s, w1_scales, nc.sync)
         n2_t = load_list("n2_t", n2)
         n1_t = load_list("n1_t", n1)
         load_words(w2w, w2_words)
@@ -74,95 +70,108 @@ def tile_picked_kqratioovercmp_none_po_kernel(
         n4_t = load_list("n4_t", n4)
         n6_t = load_list("n6_t", n6)
         n5_t = load_list("n5_t", n5)
-        gb_t = load_gain("gb_t", gb)
-        ga_t = load_gain("ga_t", ga)
-        half = sb("half", [P, 1], F32)
+        ident = sb("ident", [P, P], F32)
+        make_identity(nc, ident[:])
+        tiny = sb("tiny", [P, 1], F32)
+        nc.gpsimd.memset(tiny[:], 2.0**-60)
+        half = sb("half", [P, W], F32)
         nc.gpsimd.memset(half[:], 0.5)
 
         def deal(name, words, scales):
             dw = sb(name + "_dw", [P, PACK, P], U32)
             ds = sb(name + "_ds", [P, PACK, P], U8)
             nc.vector.tensor_copy(
-                dw[:].bitcast(I32).rearrange("p t m -> p m t"),
-                words[:].bitcast(I32).rearrange("p (m t) -> p m t", t=PACK),
+                dw[:].bitcast(I32).rearrange("p t (q j) -> p t q j", j=8),
+                words[:].bitcast(I32).rearrange("p (q t j) -> p t q j", t=PACK, j=8),
             )
             nc.vector.tensor_copy(
-                ds[:].rearrange("p t m -> p m t"), scales[:].rearrange("p (m t) -> p m t", t=PACK)
+                ds[:].bitcast(I32).rearrange("p t (q j) -> p t q j", j=2),
+                scales[:].bitcast(I32).rearrange("p (q t j) -> p t q j", t=PACK, j=2),
             )
             return dw, ds
 
-        def pick(name, lst):
-            gs = sb(name + "_gs", [P, S], U8)
-            gw = sb(name + "_gw", [P, S], U32)
-            nc.vector.tensor_copy(gs[:], xs[:].indirect(lst[:]))
-            nc.vector.tensor_copy(gw[:], xw[:].indirect(lst[:]))
-            return gw, gs
+        def pick(name, table, lst, dtype, tag=None):
+            g = sb(name, [P, S], dtype, tag)
+            nc.vector.tensor_copy(g[:], table[:].indirect(lst[:]))
+            return g
 
-        def product(lw, ls, rw, rs):
+        def product(lw, ls, rw, rs, n=512):
             acc = psum.tile([P, 512], F32, name="acc")
             nc.tensor.matmul_mx(
-                out=acc[:], lhsT=lw.bitcast(FP8X4), lhsT_scale=ls, rhs=rw.bitcast(FP8X4), rhs_scale=rs,
+                out=acc[:, :n], lhsT=lw.bitcast(FP8X4), lhsT_scale=ls, rhs=rw.bitcast(FP8X4), rhs_scale=rs,
                 start=True, stop=True,
             )
             return acc
 
         w1dw, w1ds = deal("w1", w1w, w1s)
-        xaw, xas = pick("xa", offs_t)
-        xbw, xbs = pick("xb", two_t)
+        xas = pick("xas", xs, offs_t, U8)
+        xbs = pick("xbs", xs, two_t, U8)
+        xaw = pick("xaw", xw, offs_t, U32)
+        xbw = pick("xbw", xw, two_t, U32, tag="w1s")
         w2dw, w2ds = deal("w2", w2w, w2s)
 
         a = []
         for t in range(PACK):
             acc = product(w1dw[:, t, :], w1ds[:, t, :], xaw[:], xas[:])
             a.append(sb(f"a{t}", [P, S], F32))
-            nc.scalar.copy(a[t][:], acc[:])
-        b, c = [], []
+            nc.scalar.activation(a[t][:], acc[:], ACT.Copy, scale=2.0)
+        bc = [sb(f"bc{t}", [P, 2 * V], F32) for t in range(PACK)]
+        c = [bc[t - 1][:, V:] for t in range(PACK)]
         for t in range(PACK):
             acc = product(w2dw[:, t, :], w2ds[:, t, :], xbw[:], xbs[:])
-            b.append(sb(f"b{t}", [P, V], F32))
-            c.append(sb(f"c{t}", [P, V], F32))
-            nc.scalar.copy(b[t][:], acc[:])
-            nc.scalar.activation(c[t][:], acc[:], ACT.Copy, scale=-0.75)
+            nc.scalar.copy(bc[t][:, :V], acc[:])
+            nc.scalar.activation(c[t], acc[:], ACT.Copy, scale=-0.75)
 
-        pa = sb("pa", [P, PACK, W], F32)
+        grows = sb("grows", [P, P], F32, tag="w2_ds")
+        nc.gpsimd.memset(grows[:], 0.0)
+        for i, g in enumerate((ga, gb)):
+            nc.sync.dma_start(
+                grows[PACK * i : PACK * (i + 1), :].rearrange("t (q j) -> t q j", j=8),
+                g.rearrange("(q t j) o -> t q (j o)", t=PACK, j=8),
+            )
+        gains_ps = psum.tile([P, 512], F32, name="acc")
+        nc.tensor.transpose(gains_ps[:, :P], grows[:], ident[:])
+        gains = sb("gains", [P, 2 * PACK], F32)
+        nc.scalar.copy(gains[:], gains_ps[:, : 2 * PACK])
+
         pb = sb("pb", [P, PACK, W], F32)
+        pa, rb = [], []
         for t in range(PACK):
+            pa.append(sb(f"pa{t}", [P, W], F32, tag="w2s" if t == 1 else None))
             nc.vector.tensor_copy(pb[:, t, :], a[t][:].indirect(n2_t[:]))
-            nc.vector.tensor_copy(pa[:, t, :], a[t][:].indirect(n1_t[:]))
-        rb = sb("rb", [P, PACK, W], F32)
-        nc.vector.tensor_tensor(rb[:], pa[:], pb[:], ALU.max)
-        size = sb("size", [P, PACK, W], F32)
+            nc.vector.tensor_copy(pa[t][:], a[t][:].indirect(n1_t[:]))
+        for t in range(PACK):
+            rb.append(sb(f"rb{t}", [P, W], F32))
+            nc.vector.tensor_tensor(rb[t][:], pa[t][:], pb[:, t, :], ALU.max)
+        size = sb("size", [P, PACK, W], F32, tag="w2_dw")
         logd = sb("logd", [P, PACK, W], F32)
         rec = sb("rec", [P, PACK, W], F32)
         nc.scalar.activation(size[:], pb[:], ACT.Abs)
-        nc.scalar.activation(logd[:], size[:], ACT.Ln, bias=half[:])
-        nc.scalar.activation(rec[:], logd[:], ACT.Exp, scale=-1.0)
+        nc.scalar.activation(logd[:], size[:], ACT.Ln, bias=tiny[:])
+        nc.scalar.activation(rec[:], logd[:], ACT.Sigmoid, scale=-1.0)
 
         z2b = sb("z2b", [P, V, PACK], BF16)
         for t in range(PACK):
             h3 = sb(f"h3_{t}", [P, V], F32)
             h4 = sb(f"h4_{t}", [P, V], F32)
-            for v0 in range(0, V, B_CHUNK):
-                cols = slice(v0, v0 + B_CHUNK)
-                lc = slice(v0 // 16, (v0 + B_CHUNK) // 16)
-                nc.vector.tensor_tensor(h3[:, cols], b[t][:].indirect(n3_t[:, lc]), c[t][:, cols], ALU.add)
-                nc.vector.tensor_tensor(h4[:, cols], b[t][:].indirect(n4_t[:, lc]), c[t][:, cols], ALU.add)
+            nc.vector.tensor_tensor(h3[:], bc[t][:].indirect(n3_t[:]), c[t], ALU.add)
+            nc.vector.tensor_tensor(h4[:], bc[t][:].indirect(n4_t[:]), c[t], ALU.add)
             m = sb(f"m{t}", [P, V], F32)
             nc.vector.tensor_tensor(m[:], h3[:], h4[:], ALU.max)
-            nc.scalar.activation(z2b[:, :, t], m[:], ACT.Copy, scale=gb_t[:, t : t + 1])
+            nc.scalar.activation(z2b[:, :, t], m[:], ACT.Copy, scale=gains[:, PACK + t : PACK + t + 1])
         z2w = sb("z2w", [P, V], U32)
         z2s = sb("z2s", [P, V], U8)
         nc.vector.quantize_mx(out=z2w[:].bitcast(FP8X4), scales=z2s[:], in_=z2b[:].rearrange("p v t -> p (v t)"))
 
         zb = [sb(f"zb{u}", [P, P, PACK], BF16) for u in range(PACK)]
         for t in range(PACK):
-            dt = sb(f"dt{t}", [P, S], F32)
-            nc.vector.tensor_copy(dt[:].indirect(n2_t[:]), rb[:, t, :])
-            nc.vector.tensor_tensor(dt[:].indirect(n1_t[:]), pa[:, t, :], rec[:, t, :], ALU.mult)
+            dt = sb(f"dt{t}", [P, S], F32, tag=f"h3_{t}")
+            nc.vector.tensor_tensor(dt[:].indirect(n2_t[:]), rb[t][:], half[:], ALU.mult)
+            nc.vector.tensor_tensor(dt[:].indirect(n1_t[:]), pa[t][:], rec[:, t, :], ALU.mult)
             for u in range(PACK):
                 nc.scalar.activation(
                     zb[u][:, :, t], dt[:].rearrange("p (m u) -> p u m", u=PACK)[:, u, :], ACT.Copy,
-                    scale=ga_t[:, t : t + 1],
+                    scale=gains[:, t : t + 1],
                 )
 
         sh = []
@@ -170,33 +179,75 @@ def tile_picked_kqratioovercmp_none_po_kernel(
             zw = sb(f"zw{u}", [P, P], U32)
             zs = sb(f"zs{u}", [P, P], U8)
             nc.vector.quantize_mx(out=zw[:].bitcast(FP8X4), scales=zs[:], in_=zb[u][:].rearrange("p m t -> p (m t)"))
-            acc = product(zw[:], zs[:], z2w[:], z2s[:])
             sh.append(sb(f"sh{u}", [P, V], F32))
-            nc.scalar.activation(sh[u][:], acc[:], ACT.Copy, scale=0.03125)
+            if u == 0:
+                lo = product(zw[:], zs[:], z2w[:, :W], z2s[:, :W], W)
+                hi = product(zw[:], zs[:], z2w[:, W:], z2s[:, W:], W)
+                nc.vector.tensor_scalar(sh[u][:, :W], lo[:, :W], 0.0625, None, ALU.mult)
+                nc.scalar.activation(sh[u][:, W:], hi[:, :W], ACT.Copy, scale=0.0625)
+            else:
+                acc = product(zw[:], zs[:], z2w[:], z2s[:])
+                nc.scalar.activation(sh[u][:], acc[:], ACT.Copy, scale=0.0625)
 
         out_rows = out_0.rearrange("(p u) v -> p u v", u=PACK)
         out_words = out_1[0].rearrange("p v r -> p (v r)").bitcast(I32)
         os_t = sb("os_t", [P, V], U8)
-        for v0, n in OUT_CHUNKS:
-            cols = slice(v0, v0 + n)
-            lc = slice(v0 // 16, (v0 + n) // 16)
-            o = sb(f"o{v0}", [P, PACK, n], F32)
-            for u in range(PACK):
-                g6 = sb(f"g6_{v0}_{u}", [P, n], F32)
-                d = sb(f"d_{v0}_{u}", [P, n], F32)
-                th = sb(f"th_{v0}_{u}", [P, n], F32)
-                nc.vector.tensor_copy(g6[:], sh[u][:].indirect(n6_t[:, lc]))
-                nc.vector.tensor_tensor(d[:], sh[u][:].indirect(n5_t[:, lc]), g6[:], ALU.subtract)
-                nc.scalar.activation(th[:], d[:], ACT.Tanh)
-                nc.vector.scalar_tensor_tensor(o[:, u, :], th[:], 1.0, sh[u][:, cols], ALU.add, ALU.mult)
-            nc.sync.dma_start(out_rows[:, :, cols], o[:])
-            ob = sb(f"ob{v0}", [P, n, PACK], BF16)
+        o = [sb(f"o{h}", [P, 2, V], F32) for h in range(2)]
+        ob = [sb(f"ob{v0}", [P, n, PACK], BF16) for v0, n in OUT_CHUNKS]
+
+        def cast_pair(h, i):
+            v0, n = OUT_CHUNKS[i]
             nc.scalar.copy(
-                ob[:].rearrange("p (c i) u -> p c u i", i=4), o[:].rearrange("p u (c i) -> p c u i", i=4)
+                ob[i][:, :, 2 * h : 2 * h + 2].rearrange("p (c i) e -> p c e i", i=4),
+                o[h][:, :, v0 : v0 + n].rearrange("p e (c i) -> p c e i", i=4),
             )
+
+        def look_up(u, v0, n, tag=None):
+            g6 = sb(f"g6_{u}_{v0}", [P, n], F32, tag)
+            nc.vector.tensor_copy(g6[:], sh[u][:].indirect(n6_t[:, v0 // 16 : (v0 + n) // 16]))
+            return g6
+
+        def gate(u, v0, n, g6):
+            d = sb(f"d_{u}_{v0}", [P, n], F32)
+            th = sb(f"th_{u}_{v0}", [P, n], F32)
+            nc.vector.tensor_tensor(d[:], sh[u][:].indirect(n5_t[:, v0 // 16 : (v0 + n) // 16]), g6[:], ALU.subtract)
+            nc.scalar.activation(th[:], d[:], ACT.Sigmoid)
+            return th
+
+        def finish(u, v0, n, th, engine):
+            engine.tensor_tensor(o[u // 2][:, u % 2, v0 : v0 + n], th[:], sh[u][:, v0 : v0 + n], ALU.mult)
+
+        def planes(i):
+            v0, n = OUT_CHUNKS[i]
+            cast_pair(1, i)
             ow = sb(f"ow{v0}", [P, n], U32)
-            nc.vector.quantize_mx(out=ow[:].bitcast(FP8X4), scales=os_t[:, cols], in_=ob[:].rearrange("p v u -> p (v u)"))
-            nc.sync.dma_start(out_words[:, cols], ow[:].bitcast(I32))
+            nc.vector.quantize_mx(
+                out=ow[:].bitcast(FP8X4), scales=os_t[:, v0 : v0 + n], in_=ob[i][:].rearrange("p v u -> p (v u)")
+            )
+            nc.sync.dma_start(out_words[:, v0 : v0 + n], ow[:].bitcast(I32))
+
+        halves = ((0, W), (W, W))
+        for u in range(PACK - 1):
+            g6 = [look_up(u, v0, n) for v0, n in halves]
+            for (v0, n), g in zip(halves, g6):
+                finish(u, v0, n, gate(u, v0, n, g), nc.gpsimd)
+            nc.sync.dma_start(out_rows[:, u, :], o[u // 2][:, u % 2, :])
+            if u == 1:
+                for i in range(len(OUT_CHUNKS)):
+                    cast_pair(0, i)
+        u = PACK - 1
+        c0, c1, c2 = OUT_CHUNKS
+        g0, g1 = look_up(u, *c0), look_up(u, *c1)
+        th0, th1 = gate(u, *c0, g0), gate(u, *c1, g1)
+        finish(u, *c0, th0, nc.vector)
+        g2 = look_up(u, *c2, tag=f"th_{u}_0")
+        finish(u, *c1, th1, nc.vector)
+        th2 = gate(u, *c2, g2)
+        planes(0)
+        finish(u, *c2, th2, nc.vector)
+        nc.sync.dma_start(out_rows[:, u, :], o[u // 2][:, u % 2, :])
+        planes(1)
+        planes(2)
         for q in range(4):
             queue = nc.scalar if q % 2 else nc.sync
             queue.dma_start(out_2[0, 4 * q : 4 * q + 4, :].bitcast(I32), os_t[32 * q : 32 * q + 4, :].bitcast(I32))

@@ -58,11 +58,11 @@ def tile_picked_kqratioovercmp_none_po_kernel(
         nc.gpsimd.memset(w2s[:].bitcast(I32), 0)
         offs_t = load_list("offs_t", offs)
         two_t = load_list("two_t", two)
-        load_words(w1w, w1_words)
+        n2_t = load_list("n2_t", n2)
         load_scales(xs, x_scales, nc.sync)
         load_words(xw, x_words)
+        load_words(w1w, w1_words)
         load_scales(w1s, w1_scales, nc.sync)
-        n2_t = load_list("n2_t", n2)
         n1_t = load_list("n1_t", n1)
         load_words(w2w, w2_words)
         load_scales(w2s, w2_scales, nc.sync)
@@ -122,23 +122,12 @@ def tile_picked_kqratioovercmp_none_po_kernel(
             nc.scalar.copy(bc[t][:, :V], acc[:])
             nc.scalar.activation(c[t], acc[:], ACT.Copy, scale=-0.75)
 
-        grows = sb("grows", [P, P], F32, tag="w2_ds")
-        nc.gpsimd.memset(grows[:], 0.0)
-        for i, g in enumerate((ga, gb)):
-            nc.sync.dma_start(
-                grows[PACK * i : PACK * (i + 1), :].rearrange("t (q j) -> t q j", j=8),
-                g.rearrange("(q t j) o -> t q (j o)", t=PACK, j=8),
-            )
-        gains_ps = psum.tile([P, 512], F32, name="acc")
-        nc.tensor.transpose(gains_ps[:, :P], grows[:], ident[:])
-        gains = sb("gains", [P, 2 * PACK], F32)
-        nc.scalar.copy(gains[:], gains_ps[:, : 2 * PACK])
-
         pb = sb("pb", [P, PACK, W], F32)
         pa, rb = [], []
         for t in range(PACK):
-            pa.append(sb(f"pa{t}", [P, W], F32, tag="w2s" if t == 1 else None))
             nc.vector.tensor_copy(pb[:, t, :], a[t][:].indirect(n2_t[:]))
+        for t in range(PACK):
+            pa.append(sb(f"pa{t}", [P, W], F32, tag="w2s" if t == 1 else None))
             nc.vector.tensor_copy(pa[t][:], a[t][:].indirect(n1_t[:]))
         for t in range(PACK):
             rb.append(sb(f"rb{t}", [P, W], F32))
@@ -150,29 +139,66 @@ def tile_picked_kqratioovercmp_none_po_kernel(
         nc.scalar.activation(logd[:], size[:], ACT.Ln, bias=tiny[:])
         nc.scalar.activation(rec[:], logd[:], ACT.Sigmoid, scale=-1.0)
 
+        grows = sb("grows", [P, P], F32, tag="w2_ds")
+        nc.gpsimd.memset(grows[:], 0.0)
+        for i, g in enumerate((ga, gb)):
+            nc.sync.dma_start(
+                grows[PACK * i : PACK * (i + 1), :].rearrange("t (q j) -> t q j", j=8),
+                g.rearrange("(q t j) o -> t q (j o)", t=PACK, j=8),
+            )
+        gains_ps = psum.tile([P, 512], F32, name="acc")
+        nc.tensor.transpose(gains_ps[:, :P], grows[:], ident[:])
+        gains = sb("gains", [P, 2 * PACK], F32, tag="logd")
+        nc.scalar.copy(gains[:], gains_ps[:, : 2 * PACK])
+
         z2b = sb("z2b", [P, V, PACK], BF16)
-        for t in range(PACK):
-            h3 = sb(f"h3_{t}", [P, V], F32)
-            h4 = sb(f"h4_{t}", [P, V], F32)
-            nc.vector.tensor_tensor(h3[:], bc[t][:].indirect(n3_t[:]), c[t], ALU.add)
-            nc.vector.tensor_tensor(h4[:], bc[t][:].indirect(n4_t[:]), c[t], ALU.add)
+        zb = [sb(f"zb{u}", [P, P, PACK], BF16) for u in range(PACK)]
+        dt, hs = {}, {}
+
+        def put_rb(t, tag=None):
+            dt[t] = sb(f"dt{t}", [P, S], F32, tag)
+            nc.vector.tensor_tensor(dt[t][:].indirect(n2_t[:]), rb[t][:], half[:], ALU.mult)
+
+        def put_ra(t):
+            nc.vector.tensor_tensor(dt[t][:].indirect(n1_t[:]), pa[t][:], rec[:, t, :], ALU.mult)
+            for u in range(PACK):
+                nc.scalar.activation(
+                    zb[u][:, :, t], dt[t][:].rearrange("p (m u) -> p u m", u=PACK)[:, u, :], ACT.Copy,
+                    scale=gains[:, t : t + 1],
+                )
+
+        def fetch_b(t, name, lst, tag=None):
+            hs[name, t] = sb(f"{name}_{t}", [P, V], F32, tag)
+            nc.vector.tensor_tensor(hs[name, t][:], bc[t][:].indirect(lst[:]), c[t], ALU.add)
+
+        def larger_b(t):
             m = sb(f"m{t}", [P, V], F32)
-            nc.vector.tensor_tensor(m[:], h3[:], h4[:], ALU.max)
+            nc.vector.tensor_tensor(m[:], hs["h3", t][:], hs["h4", t][:], ALU.max)
             nc.scalar.activation(z2b[:, :, t], m[:], ACT.Copy, scale=gains[:, PACK + t : PACK + t + 1])
+
+        put_rb(0)
+        put_rb(1)
+        put_rb(2)
+        fetch_b(0, "h3", n3_t)
+        fetch_b(0, "h4", n4_t)
+        fetch_b(1, "h3", n3_t)
+        larger_b(0)
+        fetch_b(1, "h4", n4_t)
+        fetch_b(2, "h3", n3_t)
+        larger_b(1)
+        put_ra(0)
+        put_ra(1)
+        fetch_b(2, "h4", n4_t, tag="pa0")
+        fetch_b(3, "h3", n3_t, tag="w2s")
+        larger_b(2)
+        put_ra(2)
+        fetch_b(3, "h4", n4_t, tag="h3_2")
+        put_rb(3, tag="pa2")
+        larger_b(3)
+        put_ra(3)
         z2w = sb("z2w", [P, V], U32)
         z2s = sb("z2s", [P, V], U8)
         nc.vector.quantize_mx(out=z2w[:].bitcast(FP8X4), scales=z2s[:], in_=z2b[:].rearrange("p v t -> p (v t)"))
-
-        zb = [sb(f"zb{u}", [P, P, PACK], BF16) for u in range(PACK)]
-        for t in range(PACK):
-            dt = sb(f"dt{t}", [P, S], F32, tag=f"h3_{t}")
-            nc.vector.tensor_tensor(dt[:].indirect(n2_t[:]), rb[t][:], half[:], ALU.mult)
-            nc.vector.tensor_tensor(dt[:].indirect(n1_t[:]), pa[t][:], rec[:, t, :], ALU.mult)
-            for u in range(PACK):
-                nc.scalar.activation(
-                    zb[u][:, :, t], dt[:].rearrange("p (m u) -> p u m", u=PACK)[:, u, :], ACT.Copy,
-                    scale=gains[:, t : t + 1],
-                )
 
         sh = []
         for u in range(PACK):
@@ -217,20 +243,23 @@ def tile_picked_kqratioovercmp_none_po_kernel(
         def finish(u, v0, n, th, engine):
             engine.tensor_tensor(o[u // 2][:, u % 2, v0 : v0 + n], th[:], sh[u][:, v0 : v0 + n], ALU.mult)
 
+        ow = [sb(f"ow{h}", [P, W], U32) for h in range(2)]
+
         def planes(i):
             v0, n = OUT_CHUNKS[i]
             cast_pair(1, i)
-            ow = sb(f"ow{v0}", [P, n], U32)
             nc.vector.quantize_mx(
-                out=ow[:].bitcast(FP8X4), scales=os_t[:, v0 : v0 + n], in_=ob[i][:].rearrange("p v u -> p (v u)")
+                out=ow[v0 // W][:, v0 % W : v0 % W + n].bitcast(FP8X4), scales=os_t[:, v0 : v0 + n],
+                in_=ob[i][:].rearrange("p v u -> p (v u)"),
             )
-            nc.sync.dma_start(out_words[:, v0 : v0 + n], ow[:].bitcast(I32))
+            if (v0 + n) % W == 0:
+                nc.sync.dma_start(out_words[:, v0 + n - W : v0 + n], ow[v0 // W][:].bitcast(I32))
 
         halves = ((0, W), (W, W))
         for u in range(PACK - 1):
             g6 = [look_up(u, v0, n) for v0, n in halves]
             for (v0, n), g in zip(halves, g6):
-                finish(u, v0, n, gate(u, v0, n, g), nc.gpsimd)
+                finish(u, v0, n, gate(u, v0, n, g), nc.vector)
             nc.sync.dma_start(out_rows[:, u, :], o[u // 2][:, u % 2, :])
             if u == 1:
                 for i in range(len(OUT_CHUNKS)):

from contextlib import ExitStack

import concourse.mybir as mybir
from concourse.masks import make_identity

K, T, S, V, H, W = 512, 2048, 512, 512, 512, 256
FLOPS = 3 * 2 * 512 * 512 * 512

F32 = mybir.dt.float32
BF16 = mybir.dt.bfloat16
I32 = mybir.dt.int32
U32 = mybir.dt.uint32
U16 = mybir.dt.uint16
U8 = mybir.dt.uint8
FP8X4 = mybir.dt.float8_e4m3fn_x4
ACT = mybir.ActivationFunctionType
ALU = mybir.AluOpType

P = 128
PACK = 4
OUT_CHUNKS = ((0, 256), (256, 128), (384, 128))
B_CHUNK = 256


def tile_picked_kqratioovercmp_none_po_kernel(
    tc, x_words, x_scales, w1_words, w1_scales, w2_words, w2_scales, ga, gb,
    offs, two, n1, n2, n3, n4, n5, n6, out_0, out_1, out_2,
):
    nc = tc.nc
    with ExitStack() as ctx:
        lists = ctx.enter_context(tc.tile_pool(name="lists", bufs=1))
        keep = ctx.enter_context(tc.tile_pool(name="keep", bufs=1))
        psum = ctx.enter_context(tc.psum_pool(name="psum", bufs=8))

        def sb(name, shape, dtype, tag=None):
            return keep.tile(shape, dtype, name=name, tag=tag or name, align_bytes=64)

        def load_list(name, src):
            t = lists.tile(list(src.shape), U16, name=name)
            nc.sync.dma_start(t[:], src)
            return t

        def load_words(t, src):
            nc.sync.dma_start(t[:].bitcast(I32), src[0].rearrange("p n r -> p (n r)").bitcast(I32))

        def load_scales(t, src, queue):
            for q in range(4):
                queue.dma_start(t[32 * q : 32 * q + 4, :].bitcast(I32), src[0, 4 * q : 4 * q + 4, :].bitcast(I32))

        xw = sb("xw", [P, T], U32)
        xs = sb("xs", [P, T], U8)
        w1w = sb("w1w", [P, H], U32)
        w1s = sb("w1s", [P, H], U8)
        w2w = sb("w2w", [P, H], U32)
        w2s = sb("w2s", [P, H], U8)
        nc.gpsimd.memset(xs[:].bitcast(I32), 0)
        nc.gpsimd.memset(w1s[:].bitcast(I32), 0)
        nc.gpsimd.memset(w2s[:].bitcast(I32), 0)
        offs_t = load_list("offs_t", offs)
        two_t = load_list("two_t", two)
        n2_t = load_list("n2_t", n2)
        load_scales(xs, x_scales, nc.sync)
        load_words(xw, x_words)
        load_words(w1w, w1_words)
        load_scales(w1s, w1_scales, nc.sync)
        n1_t = load_list("n1_t", n1)
        load_words(w2w, w2_words)
        load_scales(w2s, w2_scales, nc.sync)
        n3_t = load_list("n3_t", n3)
        n4_t = load_list("n4_t", n4)
        n6_t = load_list("n6_t", n6)
        n5_t = load_list("n5_t", n5)
        ident = sb("ident", [P, P], F32)
        make_identity(nc, ident[:])
        tiny = sb("tiny", [P, 1], F32)
        nc.gpsimd.memset(tiny[:], 2.0**-60)
        half = sb("half", [P, W], F32)
        nc.gpsimd.memset(half[:], 0.5)

        def deal(name, words, scales):
            dw = sb(name + "_dw", [P, PACK, P], U32)
            ds = sb(name + "_ds", [P, PACK, P], U8)
            nc.vector.tensor_copy(
                dw[:].bitcast(I32).rearrange("p t (q j) -> p t q j", j=8),
                words[:].bitcast(I32).rearrange("p (q t j) -> p t q j", t=PACK, j=8),
            )
            nc.vector.tensor_copy(
                ds[:].bitcast(I32).rearrange("p t (q j) -> p t q j", j=2),
                scales[:].bitcast(I32).rearrange("p (q t j) -> p t q j", t=PACK, j=2),
            )
            return dw, ds

        def pick(name, table, lst, dtype, tag=None):
            g = sb(name, [P, S], dtype, tag)
            nc.vector.tensor_copy(g[:], table[:].indirect(lst[:]))
            return g

        def product(lw, ls, rw, rs, n=512):
            acc = psum.tile([P, 512], F32, name="acc")
            nc.tensor.matmul_mx(
                out=acc[:, :n], lhsT=lw.bitcast(FP8X4), lhsT_scale=ls, rhs=rw.bitcast(FP8X4), rhs_scale=rs,
                start=True, stop=True,
            )
            return acc

        w1dw, w1ds = deal("w1", w1w, w1s)
        xas = pick("xas", xs, offs_t, U8)
        xbs = pick("xbs", xs, two_t, U8)
        xaw = pick("xaw", xw, offs_t, U32)
        xbw = pick("xbw", xw, two_t, U32, tag="w1s")
        w2dw, w2ds = deal("w2", w2w, w2s)

        a = []
        for t in range(PACK):
            acc = product(w1dw[:, t, :], w1ds[:, t, :], xaw[:], xas[:])
            a.append(sb(f"a{t}", [P, S], F32))
            nc.scalar.activation(a[t][:], acc[:], ACT.Copy, scale=2.0)
        bc = [sb(f"bc{t}", [P, 2 * V], F32) for t in range(PACK)]
        c = [bc[t - 1][:, V:] for t in range(PACK)]
        for t in range(PACK):
            acc = product(w2dw[:, t, :], w2ds[:, t, :], xbw[:], xbs[:])
            nc.scalar.copy(bc[t][:, :V], acc[:])
            nc.scalar.activation(c[t], acc[:], ACT.Copy, scale=-0.75)

        pb = sb("pb", [P, PACK, W], F32)
        pa, rb = [], []
        for t in range(PACK):
            nc.vector.tensor_copy(pb[:, t, :], a[t][:].indirect(n2_t[:]))
        for t in range(PACK):
            pa.append(sb(f"pa{t}", [P, W], F32, tag="w2s" if t == 1 else None))
            nc.vector.tensor_copy(pa[t][:], a[t][:].indirect(n1_t[:]))
        for t in range(PACK):
            rb.append(sb(f"rb{t}", [P, W], F32))
            nc.vector.tensor_tensor(rb[t][:], pa[t][:], pb[:, t, :], ALU.max)
        size = sb("size", [P, PACK, W], F32, tag="w2_dw")
        logd = sb("logd", [P, PACK, W], F32)
        rec = sb("rec", [P, PACK, W], F32)
        nc.scalar.activation(size[:], pb[:], ACT.Abs)
        nc.scalar.activation(logd[:], size[:], ACT.Ln, bias=tiny[:])
        nc.scalar.activation(rec[:], logd[:], ACT.Sigmoid, scale=-1.0)

        grows = sb("grows", [P, P], F32, tag="w2_ds")
        nc.gpsimd.memset(grows[:], 0.0)
        for i, g in enumerate((ga, gb)):
            nc.sync.dma_start(
                grows[PACK * i : PACK * (i + 1), :].rearrange("t (q j) -> t q j", j=8),
                g.rearrange("(q t j) o -> t q (j o)", t=PACK, j=8),
            )
        gains_ps = psum.tile([P, 512], F32, name="acc")
        nc.tensor.transpose(gains_ps[:, :P], grows[:], ident[:])
        gains = sb("gains", [P, 2 * PACK], F32, tag="logd")
        nc.scalar.copy(gains[:], gains_ps[:, : 2 * PACK])

        z2b = sb("z2b", [P, V, PACK], BF16)
        zb = [sb(f"zb{u}", [P, P, PACK], BF16) for u in range(PACK)]
        dt, hs = {}, {}

        def put_rb(t, tag=None):
            dt[t] = sb(f"dt{t}", [P, S], F32, tag)
            nc.vector.tensor_tensor(dt[t][:].indirect(n2_t[:]), rb[t][:], half[:], ALU.mult)

        def put_ra(t):
            nc.vector.tensor_tensor(dt[t][:].indirect(n1_t[:]), pa[t][:], rec[:, t, :], ALU.mult)
            for u in range(PACK):
                nc.scalar.activation(
                    zb[u][:, :, t], dt[t][:].rearrange("p (m u) -> p u m", u=PACK)[:, u, :], ACT.Copy,
                    scale=gains[:, t : t + 1],
                )

        def fetch_b(t, name, lst, tag=None):
            hs[name, t] = sb(f"{name}_{t}", [P, V], F32, tag)
            nc.vector.tensor_tensor(hs[name, t][:], bc[t][:].indirect(lst[:]), c[t], ALU.add)

        def larger_b(t):
            m = sb(f"m{t}", [P, V], F32)
            nc.vector.tensor_tensor(m[:], hs["h3", t][:], hs["h4", t][:], ALU.max)
            nc.scalar.activation(z2b[:, :, t], m[:], ACT.Copy, scale=gains[:, PACK + t : PACK + t + 1])

        put_rb(0)
        put_rb(1)
        put_rb(2)
        fetch_b(0, "h3", n3_t)
        fetch_b(0, "h4", n4_t)
        fetch_b(1, "h3", n3_t)
        larger_b(0)
        fetch_b(1, "h4", n4_t)
        fetch_b(2, "h3", n3_t)
        larger_b(1)
        put_ra(0)
        put_ra(1)
        fetch_b(2, "h4", n4_t, tag="pa0")
        fetch_b(3, "h3", n3_t, tag="w2s")
        larger_b(2)
        put_ra(2)
        fetch_b(3, "h4", n4_t, tag="h3_2")
        put_rb(3, tag="pa2")
        larger_b(3)
        put_ra(3)
        z2w = sb("z2w", [P, V], U32)
        z2s = sb("z2s", [P, V], U8)
        nc.vector.quantize_mx(out=z2w[:].bitcast(FP8X4), scales=z2s[:], in_=z2b[:].rearrange("p v t -> p (v t)"))

        sh = []
        for u in range(PACK):
            zw = sb(f"zw{u}", [P, P], U32)
            zs = sb(f"zs{u}", [P, P], U8)
            nc.vector.quantize_mx(out=zw[:].bitcast(FP8X4), scales=zs[:], in_=zb[u][:].rearrange("p m t -> p (m t)"))
            sh.append(sb(f"sh{u}", [P, V], F32))
            if u == 0:
                lo = product(zw[:], zs[:], z2w[:, :W], z2s[:, :W], W)
                hi = product(zw[:], zs[:], z2w[:, W:], z2s[:, W:], W)
                nc.vector.tensor_scalar(sh[u][:, :W], lo[:, :W], 0.0625, None, ALU.mult)
                nc.scalar.activation(sh[u][:, W:], hi[:, :W], ACT.Copy, scale=0.0625)
            else:
                acc = product(zw[:], zs[:], z2w[:], z2s[:])
                nc.scalar.activation(sh[u][:], acc[:], ACT.Copy, scale=0.0625)

        out_rows = out_0.rearrange("(p u) v -> p u v", u=PACK)
        out_words = out_1[0].rearrange("p v r -> p (v r)").bitcast(I32)
        os_t = sb("os_t", [P, V], U8)
        o = [sb(f"o{h}", [P, 2, V], F32) for h in range(2)]
        ob = [sb(f"ob{v0}", [P, n, PACK], BF16) for v0, n in OUT_CHUNKS]

        def cast_pair(h, i):
            v0, n = OUT_CHUNKS[i]
            nc.scalar.copy(
                ob[i][:, :, 2 * h : 2 * h + 2].rearrange("p (c i) e -> p c e i", i=4),
                o[h][:, :, v0 : v0 + n].rearrange("p e (c i) -> p c e i", i=4),
            )

        def look_up(u, v0, n, tag=None):
            g6 = sb(f"g6_{u}_{v0}", [P, n], F32, tag)
            nc.vector.tensor_copy(g6[:], sh[u][:].indirect(n6_t[:, v0 // 16 : (v0 + n) // 16]))
            return g6

        def gate(u, v0, n, g6):
            d = sb(f"d_{u}_{v0}", [P, n], F32)
            th = sb(f"th_{u}_{v0}", [P, n], F32)
            nc.vector.tensor_tensor(d[:], sh[u][:].indirect(n5_t[:, v0 // 16 : (v0 + n) // 16]), g6[:], ALU.subtract)
            nc.scalar.activation(th[:], d[:], ACT.Sigmoid)
            return th

        def finish(u, v0, n, th, engine):
            engine.tensor_tensor(o[u // 2][:, u % 2, v0 : v0 + n], th[:], sh[u][:, v0 : v0 + n], ALU.mult)

        ow = [sb(f"ow{h}", [P, W], U32) for h in range(2)]

        def planes(i):
            v0, n = OUT_CHUNKS[i]
            cast_pair(1, i)
            nc.vector.quantize_mx(
                out=ow[v0 // W][:, v0 % W : v0 % W + n].bitcast(FP8X4), scales=os_t[:, v0 : v0 + n],
                in_=ob[i][:].rearrange("p v u -> p (v u)"),
            )
            if (v0 + n) % W == 0:
                nc.sync.dma_start(out_words[:, v0 + n - W : v0 + n], ow[v0 // W][:].bitcast(I32))

        halves = ((0, W), (W, W))
        for u in range(PACK - 1):
            g6 = [look_up(u, v0, n) for v0, n in halves]
            for (v0, n), g in zip(halves, g6):
                finish(u, v0, n, gate(u, v0, n, g), nc.vector)
            nc.sync.dma_start(out_rows[:, u, :], o[u // 2][:, u % 2, :])
            if u == 1:
                for i in range(len(OUT_CHUNKS)):
                    cast_pair(0, i)
        u = PACK - 1
        c0, c1, c2 = OUT_CHUNKS
        g0, g1 = look_up(u, *c0), look_up(u, *c1)
        th0, th1 = gate(u, *c0, g0), gate(u, *c1, g1)
        finish(u, *c0, th0, nc.vector)
        g2 = look_up(u, *c2, tag=f"th_{u}_0")
        finish(u, *c1, th1, nc.vector)
        th2 = gate(u, *c2, g2)
        planes(0)
        finish(u, *c2, th2, nc.vector)
        nc.sync.dma_start(out_rows[:, u, :], o[u // 2][:, u % 2, :])
        planes(1)
        planes(2)
        for q in range(4):
            queue = nc.scalar if q % 2 else nc.sync
            queue.dma_start(out_2[0, 4 * q : 4 * q + 4, :].bitcast(I32), os_t[32 * q : 32 * q + 4, :].bitcast(I32))
